import numpy as np
import ml_dtypes


def mxq(x, axis, fmt="e4m3"):
    dtype, down = {"e4m3": (ml_dtypes.float8_e4m3fn, 7), "e5m2": (ml_dtypes.float8_e5m2, 14)}[fmt]
    v = np.moveaxis(np.asarray(x, np.float32).astype(ml_dtypes.bfloat16).astype(np.float64), axis, -1)
    blocks = v.reshape(v.shape[:-1] + (-1, 32))
    amax = np.abs(blocks).max(-1, keepdims=True)
    byte = np.maximum(np.where(amax > 0, np.frexp(amax)[1] - 1 + 127, 0) - down, 1)
    scale = np.exp2(byte - 127.0)
    codes = (blocks / scale).astype(np.float32).astype(dtype).astype(np.float64)
    return np.moveaxis((codes * scale).reshape(v.shape), -1, axis)


WIDE = False


def mx_kscale(k):
    if not WIDE:
        return np.ones(k)
    levels = np.array([30, -30])
    if k % 512:
        return np.exp2(np.random.permutation(np.resize(levels, k // 32))).repeat(32)
    a = np.empty((k // 512, 16))
    for p in range(k // 512):
        a[p, :8] = np.random.permutation(np.resize(levels, 8))
        for g in range(8):
            far = levels[np.abs(levels - a[p, g]) >= 10]
            a[p, g + 8] = far[np.random.randint(len(far))]
    return np.exp2(a.ravel()).repeat(32)


def f64(x):
    return np.asarray(x).astype(np.float64)


def striped(idx):
    return np.tile(np.asarray(idx).reshape(-1, 16).T, (8, 1)).astype(np.uint16)


def unstriped(offs):
    return offs[:16].T.reshape(-1).astype(np.int64)


E2M1 = np.array([0.0, 0.5, 1.0, 1.5, 2.0, 3.0, 4.0, 6.0, -0.0, -0.5, -1.0, -1.5, -2.0, -3.0, -4.0, -6.0])


def pack_weight(w, fmt):
    k, n = w.shape
    w = f64(np.asarray(w, np.float32).astype(ml_dtypes.bfloat16)).reshape(k // 32, 32, n)
    amax = np.abs(w).max(1)
    if fmt == "e4m3":
        byte = np.frexp(amax)[1] - 1 + 127 - 7
    else:
        mant, ex = np.frexp(amax / 6.0)
        byte = np.where(mant > 0.5, ex, ex - 1) + 127
    byte = np.clip(np.where(amax > 0, byte, 1), 1, 254)
    scaled = (w * np.exp2(127.0 - byte)[:, None, :]).reshape(k, n).astype(np.float32)
    by_word = np.ascontiguousarray(scaled.reshape(k // 512, 128, 4, n).transpose(0, 1, 3, 2))
    if fmt == "e4m3":
        words = by_word.astype(ml_dtypes.float8_e4m3fn).view(np.uint8)
    else:
        c = by_word.astype(ml_dtypes.float4_e2m1fn).view(np.uint8) & 0xF
        words = (c[..., 0::2] | (c[..., 1::2] << 4)).reshape(k // 512, 128, 2 * n)
    return np.ascontiguousarray(words), np.ascontiguousarray(byte.astype(np.uint8).reshape(k // 512, 16, n))


def unpack_weight(words, scales, fmt):
    g, _, n = scales.shape
    words = np.ascontiguousarray(words).reshape(g, 128, n, -1)
    if fmt == "e4m3":
        vals = words.view(ml_dtypes.float8_e4m3fn).astype(np.float64)
    else:
        nib = np.empty((g, 128, n, 4), np.uint8)
        nib[..., 0::2] = words & 0xF
        nib[..., 1::2] = words >> 4
        vals = E2M1[nib]
    vals = vals * np.repeat(np.exp2(scales.astype(np.float64) - 127.0), 8, axis=1)[..., None]
    return vals.transpose(0, 1, 3, 2).reshape(g * 512, n)


def sigmoid(v):
    return 1.0 / (1.0 + np.exp(-v))


K, T, J, R, F, Z, O, N, S = 512, 1024, 256, 512, 512, 1024, 128, 256, 1024


def setup_inputs():
    n = np.random.standard_normal
    idx = np.random.permutation(T)[:J]
    idx2 = np.random.permutation(Z)[:J]
    idx3 = np.random.permutation(J)[:O]
    idx4 = np.random.permutation(J)[:O]
    idx5 = np.random.permutation(J)[:O]
    idx6 = np.random.permutation(J)[:O]
    idx7 = np.random.permutation(S)[:N]
    ff = mx_kscale(F)
    fk = mx_kscale(K)
    fr = mx_kscale(R)
    xop = pack_weight(n((F, Z)) / ff[:, None], "e4m3")
    wp = pack_weight(n((K, R)) * 1 / np.sqrt(K) / fk[:, None], "e4m3")
    w2p = pack_weight(n((F, R)) * 1 / np.sqrt(F) * ff[:, None], "e2m1")
    vsp = pack_weight(n((R, S)) * 1 / np.sqrt(R) / fr[:, None], "e2m1")
    return {
        "xo_words": xop[0],
        "xo_scales": xop[1],
        "cq": (np.random.randint(-7, 8, (K, T)).astype(np.float64)).astype(np.float32),
        "gs": (np.random.uniform(0.1, 0.4, (K, 1)) * fk[:, None]).astype(np.float32),
        "w_words": wp[0],
        "w_scales": wp[1],
        "w2_words": w2p[0],
        "w2_scales": w2p[1],
        "sa": (np.random.uniform(0.5, 1.6, (R, 1)) * fr[:, None]).astype(np.float32),
        "sb": (np.random.uniform(0.5, 1.6, (R, 1)) * fr[:, None]).astype(np.float32),
        "bg": (np.random.uniform(-2.0, 2.0, (R, 1))).astype(np.float32),
        "bh": (np.random.uniform(-2.0, 2.0, (R, 1))).astype(np.float32),
        "vs_words": vsp[0],
        "vs_scales": vsp[1],
        "offs": striped(idx),
        "offs2": striped(idx2),
        "offs3": striped(idx3),
        "offs4": striped(idx4),
        "offs5": striped(idx5),
        "offs6": striped(idx6),
        "offs7": striped(idx7),
    }


def reference(xo_words, xo_scales, cq, gs, w_words, w_scales, w2_words, w2_scales, sa, sb, bg, bh, vs_words, vs_scales, offs, offs2, offs3, offs4, offs5, offs6, offs7):
    idx = unstriped(offs)
    idx2 = unstriped(offs2)
    idx3 = unstriped(offs3)
    idx4 = unstriped(offs4)
    idx5 = unstriped(offs5)
    idx6 = unstriped(offs6)
    idx7 = unstriped(offs7)
    xou = unpack_weight(xo_words, xo_scales, "e4m3")
    wu = unpack_weight(w_words, w_scales, "e4m3")
    w2u = unpack_weight(w2_words, w2_scales, "e2m1")
    vsu = unpack_weight(vs_words, vs_scales, "e2m1")
    x1 = f64(cq)[:, idx] * f64(gs)
    x1q = mxq(x1, 0, "e4m3")
    a = wu.T @ x1q
    xoidx2g = xou[:, idx2]
    b = w2u.T @ xoidx2g
    lb = b[:, 0:1]
    la = a[:, 0:1]
    u1 = a[:, idx3] * f64(sa) * sigmoid(a[:, idx4] * lb + f64(bg))
    u2 = b[:, idx5] * f64(sb) * sigmoid(b[:, idx6] * la + f64(bh))
    hid = np.abs(u1 - u2)
    vsidx7g = vsu[:, idx7]
    hidq = mxq(hid, 0, "e5m2")
    y = vsidx7g.T @ hidq
    return y

@@ -1,0 +1,219 @@
+from contextlib import ExitStack
+
+import concourse.mybir as mybir
+
+K, T, J, R, F, Z, O, N, S = 512, 1024, 256, 512, 512, 1024, 128, 256, 1024
+FLOPS = 2 * K * R * J + 2 * F * R * J + 2 * R * N * O
+
+F32 = mybir.dt.float32
+BF16 = mybir.dt.bfloat16
+I32 = mybir.dt.int32
+U32 = mybir.dt.uint32
+U16 = mybir.dt.uint16
+U8 = mybir.dt.uint8
+E4M3X4 = mybir.dt.float8_e4m3fn_x4
+E5M2X4 = mybir.dt.float8_e5m2_x4
+E2M1X4 = mybir.dt.float4_e2m1fn_x4
+ACT = mybir.ActivationFunctionType
+ALU = mybir.AluOpType
+
+P = 128
+PACK = 4
+QUADS = 4
+
+
+def tile_list_slopeboth_codednote_store_plain_kernel(
+    tc, xo_words, xo_scales, cq, gs, w_words, w_scales, w2_words, w2_scales, sa, sb, bg, bh,
+    vs_words, vs_scales, offs, offs2, offs3, offs4, offs5, offs6, offs7, out,
+):
+    nc = tc.nc
+    with ExitStack() as ctx:
+        keep = ctx.enter_context(tc.tile_pool(name="keep", bufs=1))
+        psum = ctx.enter_context(tc.psum_pool(name="psum", bufs=1))
+
+        def load_list(src, name):
+            tile = keep.tile([P, src.shape[1]], U16, name=name)
+            nc.sync.dma_start(tile[:], src)
+            return tile
+
+        def load_per_row(src, name, queue):
+            tile = keep.tile([P, PACK], F32, name=name)
+            queue.dma_start(out=tile[:], in_=src.rearrange("(p t) o -> p (t o)", t=PACK))
+            return tile
+
+        def load_scale_rows(src, name, queue):
+            tile = keep.tile([PACK, QUADS, src.shape[2] // 4], I32, name=name)
+            queue.dma_start(out=tile[:], in_=src[0].bitcast(I32).rearrange("(q r) c -> r q c", r=PACK))
+            return tile
+
+        def zero_plane(width, name):
+            plane = keep.tile([P, width], U8, name=name, align_bytes=64)
+            nc.vector.memset(plane[:].bitcast(U32), 0)
+            return plane
+
+        def spread_scale_rows(plane, rows):
+            for q in range(QUADS):
+                nc.vector.tensor_copy(out=plane[32 * q : 32 * q + PACK, :].bitcast(I32), in_=rows[:, q, :])
+
+        def load_words(src, width, dtype, name, queue):
+            tile = keep.tile([P, width], dtype, name=name, align_bytes=64)
+            queue.dma_start(out=tile[:].bitcast(I32), in_=src.bitcast(I32))
+            return tile
+
+        def deal(copy, src, dtype, name):
+            tile = keep.tile([P, PACK, P], dtype, name=name, align_bytes=64)
+            copy(out=tile[:].rearrange("p t m -> p m t"), in_=src[:].rearrange("p (m t) -> p m t", t=PACK))
+            return tile
+
+        def gather_bytes(src, offsets, dtype, name, tag=""):
+            tile = keep.tile([P, 16 * offsets.shape[1]], dtype, name=name, tag=tag, align_bytes=64)
+            nc.vector.tensor_copy(out=tile[:], in_=src[:].indirect(offsets[:]))
+            return tile
+
+        xo_rows = load_scale_rows(xo_scales, "xo_rows", nc.sync)
+        w2_rows = load_scale_rows(w2_scales, "w2_rows", nc.sync)
+        list2 = load_list(offs2, "list2")
+        list1 = load_list(offs, "list1")
+        list7 = load_list(offs7, "list7")
+        xo_w = load_words(xo_words[0].rearrange("p n t -> p (n t)"), Z, U32, "xo_w", nc.scalar)
+        w2_w = load_words(w2_words[0], R, U16, "w2_w", nc.scalar)
+        w_w = load_words(w_words[0].rearrange("p n t -> p (n t)"), R, U32, "w_w", nc.scalar)
+        cq_rows = cq.rearrange("(p t) c -> t p c", t=PACK)
+        cq_t = []
+        for t in range(PACK):
+            tile = keep.tile([P, T], F32, name="cq%d" % t)
+            nc.sync.dma_start(out=tile[:], in_=cq_rows[t])
+            cq_t.append(tile)
+        vs_w = load_words(vs_words[0], S, U16, "vs_w", nc.sync)
+        list5 = load_list(offs5, "list5")
+        list3 = load_list(offs3, "list3")
+        sa_t = load_per_row(sa, "sa_t", nc.sync)
+        list4 = load_list(offs4, "list4")
+        bg_t = load_per_row(bg, "bg_t", nc.sync)
+        list6 = load_list(offs6, "list6")
+        gs_t = load_per_row(gs, "gs_t", nc.gpsimd)
+        w_rows = load_scale_rows(w_scales, "w_rows", nc.gpsimd)
+        vs_rows = load_scale_rows(vs_scales, "vs_rows", nc.gpsimd)
+        sb_t = load_per_row(sb, "sb_t", nc.gpsimd)
+        bh_t = load_per_row(bh, "bh_t", nc.gpsimd)
+        xo_plane = zero_plane(Z, "xo_plane")
+        w2_plane = zero_plane(R, "w2_plane")
+        w_plane = zero_plane(R, "w_plane")
+        vs_plane = zero_plane(S, "vs_plane")
+
+        spread_scale_rows(xo_plane, xo_rows)
+        spread_scale_rows(w2_plane, w2_rows)
+        xo_gs = gather_bytes(xo_plane, list2, U8, "xo_gs")
+        xo_gw = gather_bytes(xo_w, list2, U32, "xo_gw")
+        w2_ds = deal(nc.vector.tensor_copy, w2_plane, U8, "w2_ds")
+        w2_dw = deal(nc.vector.tensor_copy, w2_w, U16, "w2_dw")
+        w_dw = deal(nc.scalar.copy, w_w, U32, "w_dw")
+
+        b_banks = [psum.tile([P, 2, J], F32, name="b_bank%d" % h) for h in range(2)]
+        for t in range(PACK):
+            nc.tensor.matmul_mx(
+                out=b_banks[t // 2][:, t % 2, :],
+                lhsT=w2_dw[:, t, :].bitcast(E2M1X4), lhsT_scale=w2_ds[:, t, :],
+                rhs=xo_gw[:].bitcast(E4M3X4), rhs_scale=xo_gs[:],
+                start=True, stop=True,
+            )
+        b_t = []
+        for t in range(PACK):
+            tile = keep.tile([P, J], F32, name="b%d" % t)
+            nc.vector.tensor_copy(out=tile[:], in_=b_banks[t // 2][:, t % 2, :])
+            b_t.append(tile)
+
+        spread_scale_rows(w_plane, w_rows)
+        w_ds = deal(nc.vector.tensor_copy, w_plane, U8, "w_ds")
+        spread_scale_rows(vs_plane, vs_rows)
+        vs_gs = gather_bytes(vs_plane, list7, U8, "vs_gs")
+
+        x1 = keep.tile([P, PACK, J], BF16, name="x1", tag="picks")
+        gates = [keep.tile([P, 2, O], F32, name="gates%d" % t) for t in range(PACK)]
+        for t in range(PACK):
+            nc.scalar.activation(
+                out=x1[:, t, :], in_=cq_t[t][:].indirect(list1[:]), func=ACT.Copy, scale=gs_t[:, t : t + 1]
+            )
+
+        x1_woven = keep.tile([P, J, PACK], BF16, name="x1_woven", tag="woven", align_bytes=64)
+        x1_codes = keep.tile([P, J], U32, name="x1_codes", align_bytes=64)
+        x1_plane = keep.tile([P, J], U8, name="x1_plane", align_bytes=64)
+        half = J // 2
+        for h, copy in enumerate((nc.vector.tensor_copy, nc.scalar.copy)):
+            cols = slice(h * half, (h + 1) * half)
+            copy(out=x1_woven[:, cols, :], in_=x1[:, :, cols].rearrange("p t j -> p j t"))
+        for h in range(2):
+            cols = slice(h * half, (h + 1) * half)
+            nc.vector.quantize_mx(
+                out=x1_codes[:, cols].bitcast(E4M3X4), scales=x1_plane[:, cols],
+                in_=x1_woven[:, cols, :].rearrange("p j t -> p (j t)"),
+            )
+
+        vals = keep.tile([P, PACK, 2, O], F32, name="vals", tag="picks")
+        for t in range(PACK):
+            nc.scalar.activation(
+                out=vals[:, t, 1, :], in_=b_t[t][:].indirect(list5[:]), func=ACT.Copy, scale=sb_t[:, t : t + 1]
+            )
+
+        a_banks = [psum.tile([P, J], F32, name="a_bank%d" % t) for t in range(PACK)]
+        for t in range(PACK):
+            nc.tensor.matmul_mx(
+                out=a_banks[t][:],
+                lhsT=w_dw[:, t, :].bitcast(E4M3X4), lhsT_scale=w_ds[:, t, :],
+                rhs=x1_codes[:].bitcast(E4M3X4), rhs_scale=x1_plane[:],
+                start=True, stop=True,
+            )
+        vs_gw = gather_bytes(vs_w, list7, U16, "vs_gw", tag="woven")
+
+        diff = keep.tile([P, PACK, O], F32, name="diff")
+        a_t = []
+        for t in range(PACK):
+            tile = keep.tile([P, J], F32, name="a%d" % t)
+            copy = nc.scalar.copy if t == 0 else nc.vector.tensor_copy
+            copy(out=tile[:], in_=a_banks[t][:])
+            a_t.append(tile)
+        for t in range(PACK):
+            nc.scalar.activation(
+                out=vals[:, t, 0, :], in_=a_t[t][:].indirect(list3[:]), func=ACT.Copy, scale=sa_t[:, t : t + 1]
+            )
+            nc.scalar.activation(
+                out=gates[t][:, 0, :], in_=a_t[t][:].indirect(list4[:]), func=ACT.Sigmoid,
+                scale=b_t[t][:, 0:1], bias=bg_t[:, t : t + 1],
+            )
+            nc.scalar.activation(
+                out=gates[t][:, 1, :], in_=b_t[t][:].indirect(list6[:]), func=ACT.Sigmoid,
+                scale=a_t[t][:, 0:1], bias=bh_t[:, t : t + 1],
+            )
+            u = keep.tile([P, 2, O], F32, name="u%d" % t)
+            if t < PACK - 1:
+                nc.vector.tensor_tensor(out=u[:], in0=vals[:, t, :, :], in1=gates[t][:], op=ALU.mult)
+            else:
+                for s in range(2):
+                    nc.vector.tensor_tensor(out=u[:, s, :], in0=vals[:, t, s, :], in1=gates[t][:, s, :], op=ALU.mult)
+            nc.vector.tensor_tensor(out=diff[:, t, :], in0=u[:, 0, :], in1=u[:, 1, :], op=ALU.subtract)
+
+        hid = keep.tile([P, O, PACK], BF16, name="hid", align_bytes=64)
+        first, second = slice(0, O // 2), slice(O // 2, O)
+        diff_first = diff[:, :, first].rearrange("p t o -> p o t")
+        nc.vector.scalar_tensor_tensor(
+            out=hid[:, first, :], in0=diff_first, scalar=-1.0, in1=diff_first, op0=ALU.mult, op1=ALU.max
+        )
+        nc.scalar.activation(out=hid[:, second, :], in_=diff[:, :, second].rearrange("p t o -> p o t"), func=ACT.Abs)
+        hid_codes = keep.tile([P, O], U32, name="hid_codes", align_bytes=64)
+        hid_plane = keep.tile([P, O], U8, name="hid_plane", align_bytes=64)
+        nc.vector.quantize_mx(
+            out=hid_codes[:].bitcast(E5M2X4), scales=hid_plane[:], in_=hid[:].rearrange("p o t -> p (o t)")
+        )
+
+        for h, (copy, queue) in enumerate(((nc.vector.tensor_copy, nc.sync), (nc.scalar.copy, nc.scalar))):
+            rows = slice(h * P, (h + 1) * P)
+            bank = psum.tile([P, O], F32, name="y_bank%d" % h)
+            nc.tensor.matmul_mx(
+                out=bank[:],
+                lhsT=vs_gw[:, rows].bitcast(E2M1X4), lhsT_scale=vs_gs[:, rows],
+                rhs=hid_codes[:].bitcast(E5M2X4), rhs_scale=hid_plane[:],
+                start=True, stop=True,
+            )
+            y = keep.tile([P, O], F32, name="y%d" % h)
+            copy(out=y[:], in_=bank[:])
+            queue.dma_start(out=out[rows, :], in_=y[:])

@@ -96,6 +96,11 @@ def tile_list_slopeboth_codednote_store_plain_kernel(
         vs_rows = load_scale_rows(vs_scales, "vs_rows", nc.gpsimd)
         sb_t = load_per_row(sb, "sb_t", nc.gpsimd)
         bh_t = load_per_row(bh, "bh_t", nc.gpsimd)
+
+        warm = keep.tile([P, 2], F32, name="warm")
+        nc.vector.memset(warm[:, 0:1], 0.0)
+        nc.scalar.activation(out=warm[:, 1:2], in_=warm[:, 0:1], func=ACT.Sigmoid)
+
         xo_plane = zero_plane(Z, "xo_plane")
         w2_plane = zero_plane(R, "w2_plane")
         w_plane = zero_plane(R, "w_plane")

@@ -41,14 +41,12 @@ def tile_list_slopeboth_codednote_store_plain_kernel(
             queue.dma_start(out=tile[:], in_=src.rearrange("(p t) o -> p (t o)", t=PACK))
             return tile
 
-        def load_scale_rows(src, name, queue):
-            tile = keep.tile([PACK, QUADS, src.shape[2] // 4], I32, name=name)
-            queue.dma_start(out=tile[:], in_=src[0].bitcast(I32).rearrange("(q r) c -> r q c", r=PACK))
-            return tile
+        def load_scale_rows(dst, src):
+            nc.sync.dma_start(out=dst, in_=src[0].bitcast(I32).rearrange("(q r) c -> r q c", r=PACK))
 
-        def zero_plane(width, name):
+        def zero_plane(width, name, engine):
             plane = keep.tile([P, width], U8, name=name, align_bytes=64)
-            nc.vector.memset(plane[:].bitcast(U32), 0)
+            engine.memset(plane[:].bitcast(U32), 0)
             return plane
 
         def spread_scale_rows(plane, rows):
@@ -62,7 +60,7 @@ def tile_list_slopeboth_codednote_store_plain_kernel(
 
         def deal(copy, src, dtype, name):
             tile = keep.tile([P, PACK, P], dtype, name=name, align_bytes=64)
-            copy(out=tile[:].rearrange("p t m -> p m t"), in_=src[:].rearrange("p (m t) -> p m t", t=PACK))
+            copy(out=tile[:].rearrange("p t m -> p m t"), in_=src.rearrange("p (m t) -> p m t", t=PACK))
             return tile
 
         def gather_bytes(src, offsets, dtype, name, tag=""):
@@ -70,11 +68,13 @@ def tile_list_slopeboth_codednote_store_plain_kernel(
             nc.vector.tensor_copy(out=tile[:], in_=src[:].indirect(offsets[:]))
             return tile
 
-        xo_rows = load_scale_rows(xo_scales, "xo_rows", nc.sync)
-        w2_rows = load_scale_rows(w2_scales, "w2_rows", nc.sync)
+        xo_rows = keep.tile([PACK, QUADS, Z // 4], I32, name="xo_rows")
+        load_scale_rows(xo_rows[:], xo_scales)
+        ww_rows = keep.tile([PACK, QUADS, 2 * R // 4], I32, name="ww_rows")
+        load_scale_rows(ww_rows[:, :, : R // 4], w2_scales)
+        load_scale_rows(ww_rows[:, :, R // 4 :], w_scales)
         list2 = load_list(offs2, "list2")
         list1 = load_list(offs, "list1")
-        list7 = load_list(offs7, "list7")
         xo_w = load_words(xo_words[0].rearrange("p n t -> p (n t)"), Z, U32, "xo_w", nc.scalar)
         w2_w = load_words(w2_words[0], R, U16, "w2_w", nc.scalar)
         w_w = load_words(w_words[0].rearrange("p n t -> p (n t)"), R, U32, "w_w", nc.scalar)
@@ -84,35 +84,37 @@ def tile_list_slopeboth_codednote_store_plain_kernel(
             tile = keep.tile([P, T], F32, name="cq%d" % t)
             nc.sync.dma_start(out=tile[:], in_=cq_rows[t])
             cq_t.append(tile)
-        vs_w = load_words(vs_words[0], S, U16, "vs_w", nc.sync)
         list5 = load_list(offs5, "list5")
+        vs_w = load_words(vs_words[0], S, U16, "vs_w", nc.sync)
+        list7 = load_list(offs7, "list7")
         list3 = load_list(offs3, "list3")
         sa_t = load_per_row(sa, "sa_t", nc.sync)
         list4 = load_list(offs4, "list4")
         bg_t = load_per_row(bg, "bg_t", nc.sync)
         list6 = load_list(offs6, "list6")
         gs_t = load_per_row(gs, "gs_t", nc.gpsimd)
-        w_rows = load_scale_rows(w_scales, "w_rows", nc.gpsimd)
-        vs_rows = load_scale_rows(vs_scales, "vs_rows", nc.gpsimd)
         sb_t = load_per_row(sb, "sb_t", nc.gpsimd)
         bh_t = load_per_row(bh, "bh_t", nc.gpsimd)
+        vs_plane = zero_plane(S, "vs_plane", nc.gpsimd)
+        vs_rows = vs_scales[0].bitcast(I32).rearrange("(q r) c -> r q c", r=PACK)
+        for r in range(PACK):
+            nc.gpsimd.dma_start(out=vs_plane[r:P:32, :].bitcast(I32), in_=vs_rows[r])
 
         warm = keep.tile([P, 2], F32, name="warm")
         nc.vector.memset(warm[:, 0:1], 0.0)
         nc.scalar.activation(out=warm[:, 1:2], in_=warm[:, 0:1], func=ACT.Sigmoid)
 
-        xo_plane = zero_plane(Z, "xo_plane")
-        w2_plane = zero_plane(R, "w2_plane")
-        w_plane = zero_plane(R, "w_plane")
-        vs_plane = zero_plane(S, "vs_plane")
+        xo_plane = zero_plane(Z, "xo_plane", nc.vector)
+        ww_plane = zero_plane(2 * R, "ww_plane", nc.vector)
 
         spread_scale_rows(xo_plane, xo_rows)
-        spread_scale_rows(w2_plane, w2_rows)
+        spread_scale_rows(ww_plane, ww_rows)
         xo_gs = gather_bytes(xo_plane, list2, U8, "xo_gs")
         xo_gw = gather_bytes(xo_w, list2, U32, "xo_gw")
-        w2_ds = deal(nc.vector.tensor_copy, w2_plane, U8, "w2_ds")
-        w2_dw = deal(nc.vector.tensor_copy, w2_w, U16, "w2_dw")
-        w_dw = deal(nc.scalar.copy, w_w, U32, "w_dw")
+        w2_ds = deal(nc.vector.tensor_copy, ww_plane[:, :R], U8, "w2_ds")
+        w_ds = deal(nc.vector.tensor_copy, ww_plane[:, R:], U8, "w_ds")
+        w2_dw = deal(nc.scalar.copy, w2_w[:], U16, "w2_dw")
+        w_dw = deal(nc.scalar.copy, w_w[:], U32, "w_dw")
 
         b_banks = [psum.tile([P, 2, J], F32, name="b_bank%d" % h) for h in range(2)]
         for t in range(PACK):
@@ -128,11 +130,6 @@ def tile_list_slopeboth_codednote_store_plain_kernel(
             nc.vector.tensor_copy(out=tile[:], in_=b_banks[t // 2][:, t % 2, :])
             b_t.append(tile)
 
-        spread_scale_rows(w_plane, w_rows)
-        w_ds = deal(nc.vector.tensor_copy, w_plane, U8, "w_ds")
-        spread_scale_rows(vs_plane, vs_rows)
-        vs_gs = gather_bytes(vs_plane, list7, U8, "vs_gs")
-
         x1 = keep.tile([P, PACK, J], BF16, name="x1", tag="picks")
         gates = [keep.tile([P, 2, O], F32, name="gates%d" % t) for t in range(PACK)]
         for t in range(PACK):
@@ -142,7 +139,7 @@ def tile_list_slopeboth_codednote_store_plain_kernel(
 
         x1_woven = keep.tile([P, J, PACK], BF16, name="x1_woven", tag="woven", align_bytes=64)
         x1_codes = keep.tile([P, J], U32, name="x1_codes", align_bytes=64)
-        x1_plane = keep.tile([P, J], U8, name="x1_plane", align_bytes=64)
+        x1_plane = keep.tile([P, J], U8, name="x1_plane", tag="plane", align_bytes=64)
         half = J // 2
         for h, copy in enumerate((nc.vector.tensor_copy, nc.scalar.copy)):
             cols = slice(h * half, (h + 1) * half)
@@ -174,9 +171,9 @@ def tile_list_slopeboth_codednote_store_plain_kernel(
         a_t = []
         for t in range(PACK):
             tile = keep.tile([P, J], F32, name="a%d" % t)
-            copy = nc.scalar.copy if t == 0 else nc.vector.tensor_copy
-            copy(out=tile[:], in_=a_banks[t][:])
+            nc.vector.tensor_copy(out=tile[:], in_=a_banks[t][:])
             a_t.append(tile)
+        vs_gs = gather_bytes(vs_plane, list7, U8, "vs_gs", tag="plane")
         for t in range(PACK):
             nc.scalar.activation(
                 out=vals[:, t, 0, :], in_=a_t[t][:].indirect(list3[:]), func=ACT.Copy, scale=sa_t[:, t : t + 1]

@@ -20,6 +20,7 @@ ALU = mybir.AluOpType
 P = 128
 PACK = 4
 QUADS = 4
+ABS_SPLIT = 32
 
 
 def tile_list_slopeboth_codednote_store_plain_kernel(
@@ -41,17 +42,15 @@ def tile_list_slopeboth_codednote_store_plain_kernel(
             queue.dma_start(out=tile[:], in_=src.rearrange("(p t) o -> p (t o)", t=PACK))
             return tile
 
-        def load_scale_rows(dst, src):
-            nc.sync.dma_start(out=dst, in_=src[0].bitcast(I32).rearrange("(q r) c -> r q c", r=PACK))
+        def scale_rows(src):
+            return src[0].bitcast(I32).rearrange("(q r) c -> r q c", r=PACK)
 
-        def zero_plane(width, name, engine):
-            plane = keep.tile([P, width], U8, name=name, align_bytes=64)
+        def load_plane(src, name, engine, queue):
+            plane = keep.tile([P, src.shape[2]], U8, name=name, align_bytes=64)
             engine.memset(plane[:].bitcast(U32), 0)
-            return plane
-
-        def spread_scale_rows(plane, rows):
-            for q in range(QUADS):
-                nc.vector.tensor_copy(out=plane[32 * q : 32 * q + PACK, :].bitcast(I32), in_=rows[:, q, :])
+            return plane, lambda: [
+                queue.dma_start(out=plane[r:P:32, :].bitcast(I32), in_=scale_rows(src)[r]) for r in range(PACK)
+            ]
 
         def load_words(src, width, dtype, name, queue):
             tile = keep.tile([P, width], dtype, name=name, align_bytes=64)
@@ -68,59 +67,55 @@ def tile_list_slopeboth_codednote_store_plain_kernel(
             nc.vector.tensor_copy(out=tile[:], in_=src[:].indirect(offsets[:]))
             return tile
 
-        xo_rows = keep.tile([PACK, QUADS, Z // 4], I32, name="xo_rows")
-        load_scale_rows(xo_rows[:], xo_scales)
-        ww_rows = keep.tile([PACK, QUADS, 2 * R // 4], I32, name="ww_rows")
-        load_scale_rows(ww_rows[:, :, : R // 4], w2_scales)
-        load_scale_rows(ww_rows[:, :, R // 4 :], w_scales)
+        ww_rows = keep.tile([32, QUADS, R // 4], I32, name="ww_rows")
+        nc.vector.memset(ww_rows[:], 0)
+        xo_plane, load_xo_plane = load_plane(xo_scales, "xo_plane", nc.vector, nc.sync)
         list2 = load_list(offs2, "list2")
         list1 = load_list(offs, "list1")
+        nc.sync.dma_start(out=ww_rows[0:PACK], in_=scale_rows(w2_scales))
+        nc.sync.dma_start(out=ww_rows[PACK : 2 * PACK], in_=scale_rows(w_scales))
+        load_xo_plane()
         xo_w = load_words(xo_words[0].rearrange("p n t -> p (n t)"), Z, U32, "xo_w", nc.scalar)
         w2_w = load_words(w2_words[0], R, U16, "w2_w", nc.scalar)
-        w_w = load_words(w_words[0].rearrange("p n t -> p (n t)"), R, U32, "w_w", nc.scalar)
         cq_rows = cq.rearrange("(p t) c -> t p c", t=PACK)
         cq_t = []
         for t in range(PACK):
             tile = keep.tile([P, T], F32, name="cq%d" % t)
-            nc.sync.dma_start(out=tile[:], in_=cq_rows[t])
+            queue = nc.scalar if t < 2 else nc.sync
+            queue.dma_start(out=tile[:], in_=cq_rows[t])
             cq_t.append(tile)
+        w_w = load_words(w_words[0].rearrange("p n t -> p (n t)"), R, U32, "w_w", nc.sync)
         list5 = load_list(offs5, "list5")
         vs_w = load_words(vs_words[0], S, U16, "vs_w", nc.sync)
         list7 = load_list(offs7, "list7")
         list3 = load_list(offs3, "list3")
-        sa_t = load_per_row(sa, "sa_t", nc.sync)
         list4 = load_list(offs4, "list4")
-        bg_t = load_per_row(bg, "bg_t", nc.sync)
         list6 = load_list(offs6, "list6")
         gs_t = load_per_row(gs, "gs_t", nc.gpsimd)
         sb_t = load_per_row(sb, "sb_t", nc.gpsimd)
+        sa_t = load_per_row(sa, "sa_t", nc.gpsimd)
+        bg_t = load_per_row(bg, "bg_t", nc.gpsimd)
         bh_t = load_per_row(bh, "bh_t", nc.gpsimd)
-        vs_plane = zero_plane(S, "vs_plane", nc.gpsimd)
-        vs_rows = vs_scales[0].bitcast(I32).rearrange("(q r) c -> r q c", r=PACK)
-        for r in range(PACK):
-            nc.gpsimd.dma_start(out=vs_plane[r:P:32, :].bitcast(I32), in_=vs_rows[r])
+        vs_plane, load_vs_plane = load_plane(vs_scales, "vs_plane", nc.gpsimd, nc.gpsimd)
+        load_vs_plane()
 
         warm = keep.tile([P, 2], F32, name="warm")
         nc.vector.memset(warm[:, 0:1], 0.0)
         nc.scalar.activation(out=warm[:, 1:2], in_=warm[:, 0:1], func=ACT.Sigmoid)
 
-        xo_plane = zero_plane(Z, "xo_plane", nc.vector)
-        ww_plane = zero_plane(2 * R, "ww_plane", nc.vector)
-
-        spread_scale_rows(xo_plane, xo_rows)
-        spread_scale_rows(ww_plane, ww_rows)
-        xo_gs = gather_bytes(xo_plane, list2, U8, "xo_gs")
+        ww_plane = keep.tile([P, R], U8, name="ww_plane", align_bytes=64)
+        for q in range(QUADS):
+            nc.vector.tensor_copy(out=ww_plane[32 * q : 32 * (q + 1), :].bitcast(I32), in_=ww_rows[:, q, :])
         xo_gw = gather_bytes(xo_w, list2, U32, "xo_gw")
-        w2_ds = deal(nc.vector.tensor_copy, ww_plane[:, :R], U8, "w2_ds")
-        w_ds = deal(nc.vector.tensor_copy, ww_plane[:, R:], U8, "w_ds")
+        ww_ds = deal(nc.vector.tensor_copy, ww_plane[:], U8, "ww_ds")
+        xo_gs = gather_bytes(xo_plane, list2, U8, "xo_gs")
         w2_dw = deal(nc.scalar.copy, w2_w[:], U16, "w2_dw")
-        w_dw = deal(nc.scalar.copy, w_w[:], U32, "w_dw")
 
         b_banks = [psum.tile([P, 2, J], F32, name="b_bank%d" % h) for h in range(2)]
         for t in range(PACK):
             nc.tensor.matmul_mx(
                 out=b_banks[t // 2][:, t % 2, :],
-                lhsT=w2_dw[:, t, :].bitcast(E2M1X4), lhsT_scale=w2_ds[:, t, :],
+                lhsT=w2_dw[:, t, :].bitcast(E2M1X4), lhsT_scale=ww_ds[:, t, :],
                 rhs=xo_gw[:].bitcast(E4M3X4), rhs_scale=xo_gs[:],
                 start=True, stop=True,
             )
@@ -144,12 +139,21 @@ def tile_list_slopeboth_codednote_store_plain_kernel(
         for h, copy in enumerate((nc.vector.tensor_copy, nc.scalar.copy)):
             cols = slice(h * half, (h + 1) * half)
             copy(out=x1_woven[:, cols, :], in_=x1[:, :, cols].rearrange("p t j -> p j t"))
+
+        def deal_w_pair(pair):
+            tile = keep.tile([P, 2, P], U32, name="w_dw%d" % pair, align_bytes=64)
+            src = w_w[:].rearrange("p (m t) -> p m t", t=PACK)[:, :, 2 * pair : 2 * pair + 2]
+            nc.vector.tensor_copy(out=tile[:].rearrange("p t m -> p m t"), in_=src)
+            return tile
+
+        w_dw = [deal_w_pair(0)]
         for h in range(2):
             cols = slice(h * half, (h + 1) * half)
             nc.vector.quantize_mx(
                 out=x1_codes[:, cols].bitcast(E4M3X4), scales=x1_plane[:, cols],
                 in_=x1_woven[:, cols, :].rearrange("p j t -> p (j t)"),
             )
+        w_dw.append(deal_w_pair(1))
 
         vals = keep.tile([P, PACK, 2, O], F32, name="vals", tag="picks")
         for t in range(PACK):
@@ -161,7 +165,7 @@ def tile_list_slopeboth_codednote_store_plain_kernel(
         for t in range(PACK):
             nc.tensor.matmul_mx(
                 out=a_banks[t][:],
-                lhsT=w_dw[:, t, :].bitcast(E4M3X4), lhsT_scale=w_ds[:, t, :],
+                lhsT=w_dw[t // 2][:, t % 2, :].bitcast(E4M3X4), lhsT_scale=ww_ds[PACK:, t, :],
                 rhs=x1_codes[:].bitcast(E4M3X4), rhs_scale=x1_plane[:],
                 start=True, stop=True,
             )
@@ -173,7 +177,6 @@ def tile_list_slopeboth_codednote_store_plain_kernel(
             tile = keep.tile([P, J], F32, name="a%d" % t)
             nc.vector.tensor_copy(out=tile[:], in_=a_banks[t][:])
             a_t.append(tile)
-        vs_gs = gather_bytes(vs_plane, list7, U8, "vs_gs", tag="plane")
         for t in range(PACK):
             nc.scalar.activation(
                 out=vals[:, t, 0, :], in_=a_t[t][:].indirect(list3[:]), func=ACT.Copy, scale=sa_t[:, t : t + 1]
@@ -193,9 +196,11 @@ def tile_list_slopeboth_codednote_store_plain_kernel(
                 for s in range(2):
                     nc.vector.tensor_tensor(out=u[:, s, :], in0=vals[:, t, s, :], in1=gates[t][:, s, :], op=ALU.mult)
             nc.vector.tensor_tensor(out=diff[:, t, :], in0=u[:, 0, :], in1=u[:, 1, :], op=ALU.subtract)
+            if t == 0:
+                vs_gs = gather_bytes(vs_plane, list7, U8, "vs_gs", tag="plane")
 
         hid = keep.tile([P, O, PACK], BF16, name="hid", align_bytes=64)
-        first, second = slice(0, O // 2), slice(O // 2, O)
+        first, second = slice(0, ABS_SPLIT), slice(ABS_SPLIT, O)
         diff_first = diff[:, :, first].rearrange("p t o -> p o t")
         nc.vector.scalar_tensor_tensor(
             out=hid[:, first, :], in0=diff_first, scalar=-1.0, in1=diff_first, op0=ALU.mult, op1=ALU.max

from contextlib import ExitStack

import concourse.mybir as mybir

K, T, J, R, F, Z, O, N, S = 512, 1024, 256, 512, 512, 1024, 128, 256, 1024
FLOPS = 2 * K * R * J + 2 * F * R * J + 2 * R * N * O

F32 = mybir.dt.float32
BF16 = mybir.dt.bfloat16
I32 = mybir.dt.int32
U32 = mybir.dt.uint32
U16 = mybir.dt.uint16
U8 = mybir.dt.uint8
E4M3X4 = mybir.dt.float8_e4m3fn_x4
E5M2X4 = mybir.dt.float8_e5m2_x4
E2M1X4 = mybir.dt.float4_e2m1fn_x4
ACT = mybir.ActivationFunctionType
ALU = mybir.AluOpType

P = 128
PACK = 4
QUADS = 4
ABS_SPLIT = 32


def tile_list_slopeboth_codednote_store_plain_kernel(
    tc, xo_words, xo_scales, cq, gs, w_words, w_scales, w2_words, w2_scales, sa, sb, bg, bh,
    vs_words, vs_scales, offs, offs2, offs3, offs4, offs5, offs6, offs7, out,
):
    nc = tc.nc
    with ExitStack() as ctx:
        keep = ctx.enter_context(tc.tile_pool(name="keep", bufs=1))
        psum = ctx.enter_context(tc.psum_pool(name="psum", bufs=1))

        def load_list(src, name):
            tile = keep.tile([P, src.shape[1]], U16, name=name)
            nc.sync.dma_start(tile[:], src)
            return tile

        def load_per_row(src, name, queue):
            tile = keep.tile([P, PACK], F32, name=name)
            queue.dma_start(out=tile[:], in_=src.rearrange("(p t) o -> p (t o)", t=PACK))
            return tile

        def scale_rows(src):
            return src[0].bitcast(I32).rearrange("(q r) c -> r q c", r=PACK)

        def load_plane(src, name, engine, queue):
            plane = keep.tile([P, src.shape[2]], U8, name=name, align_bytes=64)
            engine.memset(plane[:].bitcast(U32), 0)
            return plane, lambda: [
                queue.dma_start(out=plane[r:P:32, :].bitcast(I32), in_=scale_rows(src)[r]) for r in range(PACK)
            ]

        def load_words(src, width, dtype, name, queue):
            tile = keep.tile([P, width], dtype, name=name, align_bytes=64)
            queue.dma_start(out=tile[:].bitcast(I32), in_=src.bitcast(I32))
            return tile

        def deal(copy, src, dtype, name):
            tile = keep.tile([P, PACK, P], dtype, name=name, align_bytes=64)
            copy(out=tile[:].rearrange("p t m -> p m t"), in_=src.rearrange("p (m t) -> p m t", t=PACK))
            return tile

        def gather_bytes(src, offsets, dtype, name, tag=""):
            tile = keep.tile([P, 16 * offsets.shape[1]], dtype, name=name, tag=tag, align_bytes=64)
            nc.vector.tensor_copy(out=tile[:], in_=src[:].indirect(offsets[:]))
            return tile

        ww_rows = keep.tile([32, QUADS, R // 4], I32, name="ww_rows")
        nc.vector.memset(ww_rows[:], 0)
        xo_plane, load_xo_plane = load_plane(xo_scales, "xo_plane", nc.vector, nc.sync)
        list2 = load_list(offs2, "list2")
        list1 = load_list(offs, "list1")
        nc.sync.dma_start(out=ww_rows[0:PACK], in_=scale_rows(w2_scales))
        nc.sync.dma_start(out=ww_rows[PACK : 2 * PACK], in_=scale_rows(w_scales))
        load_xo_plane()
        xo_w = load_words(xo_words[0].rearrange("p n t -> p (n t)"), Z, U32, "xo_w", nc.scalar)
        w2_w = load_words(w2_words[0], R, U16, "w2_w", nc.scalar)
        cq_rows = cq.rearrange("(p t) c -> t p c", t=PACK)
        cq_t = []
        for t in range(PACK):
            tile = keep.tile([P, T], F32, name="cq%d" % t)
            queue = nc.scalar if t < 2 else nc.sync
            queue.dma_start(out=tile[:], in_=cq_rows[t])
            cq_t.append(tile)
        w_w = load_words(w_words[0].rearrange("p n t -> p (n t)"), R, U32, "w_w", nc.sync)
        list5 = load_list(offs5, "list5")
        vs_w = load_words(vs_words[0], S, U16, "vs_w", nc.sync)
        list7 = load_list(offs7, "list7")
        list3 = load_list(offs3, "list3")
        list4 = load_list(offs4, "list4")
        list6 = load_list(offs6, "list6")
        gs_t = load_per_row(gs, "gs_t", nc.gpsimd)
        sb_t = load_per_row(sb, "sb_t", nc.gpsimd)
        sa_t = load_per_row(sa, "sa_t", nc.gpsimd)
        bg_t = load_per_row(bg, "bg_t", nc.gpsimd)
        bh_t = load_per_row(bh, "bh_t", nc.gpsimd)
        vs_plane, load_vs_plane = load_plane(vs_scales, "vs_plane", nc.gpsimd, nc.gpsimd)
        load_vs_plane()

        warm = keep.tile([P, 2], F32, name="warm")
        nc.vector.memset(warm[:, 0:1], 0.0)
        nc.scalar.activation(out=warm[:, 1:2], in_=warm[:, 0:1], func=ACT.Sigmoid)

        ww_plane = keep.tile([P, R], U8, name="ww_plane", align_bytes=64)
        for q in range(QUADS):
            nc.vector.tensor_copy(out=ww_plane[32 * q : 32 * (q + 1), :].bitcast(I32), in_=ww_rows[:, q, :])
        xo_gw = gather_bytes(xo_w, list2, U32, "xo_gw")
        ww_ds = deal(nc.vector.tensor_copy, ww_plane[:], U8, "ww_ds")
        xo_gs = gather_bytes(xo_plane, list2, U8, "xo_gs")
        w2_dw = deal(nc.scalar.copy, w2_w[:], U16, "w2_dw")

        b_banks = [psum.tile([P, 2, J], F32, name="b_bank%d" % h) for h in range(2)]
        for t in range(PACK):
            nc.tensor.matmul_mx(
                out=b_banks[t // 2][:, t % 2, :],
                lhsT=w2_dw[:, t, :].bitcast(E2M1X4), lhsT_scale=ww_ds[:, t, :],
                rhs=xo_gw[:].bitcast(E4M3X4), rhs_scale=xo_gs[:],
                start=True, stop=True,
            )
        b_t = []
        for t in range(PACK):
            tile = keep.tile([P, J], F32, name="b%d" % t)
            nc.vector.tensor_copy(out=tile[:], in_=b_banks[t // 2][:, t % 2, :])
            b_t.append(tile)

        x1 = keep.tile([P, PACK, J], BF16, name="x1", tag="picks")
        gates = [keep.tile([P, 2, O], F32, name="gates%d" % t) for t in range(PACK)]
        for t in range(PACK):
            nc.scalar.activation(
                out=x1[:, t, :], in_=cq_t[t][:].indirect(list1[:]), func=ACT.Copy, scale=gs_t[:, t : t + 1]
            )

        x1_woven = keep.tile([P, J, PACK], BF16, name="x1_woven", tag="woven", align_bytes=64)
        x1_codes = keep.tile([P, J], U32, name="x1_codes", align_bytes=64)
        x1_plane = keep.tile([P, J], U8, name="x1_plane", tag="plane", align_bytes=64)
        half = J // 2
        for h, copy in enumerate((nc.vector.tensor_copy, nc.scalar.copy)):
            cols = slice(h * half, (h + 1) * half)
            copy(out=x1_woven[:, cols, :], in_=x1[:, :, cols].rearrange("p t j -> p j t"))

        def deal_w_pair(pair):
            tile = keep.tile([P, 2, P], U32, name="w_dw%d" % pair, align_bytes=64)
            src = w_w[:].rearrange("p (m t) -> p m t", t=PACK)[:, :, 2 * pair : 2 * pair + 2]
            nc.vector.tensor_copy(out=tile[:].rearrange("p t m -> p m t"), in_=src)
            return tile

        w_dw = [deal_w_pair(0)]
        for h in range(2):
            cols = slice(h * half, (h + 1) * half)
            nc.vector.quantize_mx(
                out=x1_codes[:, cols].bitcast(E4M3X4), scales=x1_plane[:, cols],
                in_=x1_woven[:, cols, :].rearrange("p j t -> p (j t)"),
            )
        w_dw.append(deal_w_pair(1))

        vals = keep.tile([P, PACK, 2, O], F32, name="vals", tag="picks")
        for t in range(PACK):
            nc.scalar.activation(
                out=vals[:, t, 1, :], in_=b_t[t][:].indirect(list5[:]), func=ACT.Copy, scale=sb_t[:, t : t + 1]
            )

        a_banks = [psum.tile([P, J], F32, name="a_bank%d" % t) for t in range(PACK)]
        for t in range(PACK):
            nc.tensor.matmul_mx(
                out=a_banks[t][:],
                lhsT=w_dw[t // 2][:, t % 2, :].bitcast(E4M3X4), lhsT_scale=ww_ds[PACK:, t, :],
                rhs=x1_codes[:].bitcast(E4M3X4), rhs_scale=x1_plane[:],
                start=True, stop=True,
            )
        vs_gw = gather_bytes(vs_w, list7, U16, "vs_gw", tag="woven")

        diff = keep.tile([P, PACK, O], F32, name="diff")
        a_t = []
        for t in range(PACK):
            tile = keep.tile([P, J], F32, name="a%d" % t)
            nc.vector.tensor_copy(out=tile[:], in_=a_banks[t][:])
            a_t.append(tile)
        for t in range(PACK):
            nc.scalar.activation(
                out=vals[:, t, 0, :], in_=a_t[t][:].indirect(list3[:]), func=ACT.Copy, scale=sa_t[:, t : t + 1]
            )
            nc.scalar.activation(
                out=gates[t][:, 0, :], in_=a_t[t][:].indirect(list4[:]), func=ACT.Sigmoid,
                scale=b_t[t][:, 0:1], bias=bg_t[:, t : t + 1],
            )
            nc.scalar.activation(
                out=gates[t][:, 1, :], in_=b_t[t][:].indirect(list6[:]), func=ACT.Sigmoid,
                scale=a_t[t][:, 0:1], bias=bh_t[:, t : t + 1],
            )
            u = keep.tile([P, 2, O], F32, name="u%d" % t)
            if t < PACK - 1:
                nc.vector.tensor_tensor(out=u[:], in0=vals[:, t, :, :], in1=gates[t][:], op=ALU.mult)
            else:
                for s in range(2):
                    nc.vector.tensor_tensor(out=u[:, s, :], in0=vals[:, t, s, :], in1=gates[t][:, s, :], op=ALU.mult)
            nc.vector.tensor_tensor(out=diff[:, t, :], in0=u[:, 0, :], in1=u[:, 1, :], op=ALU.subtract)
            if t == 0:
                vs_gs = gather_bytes(vs_plane, list7, U8, "vs_gs", tag="plane")

        hid = keep.tile([P, O, PACK], BF16, name="hid", align_bytes=64)
        first, second = slice(0, ABS_SPLIT), slice(ABS_SPLIT, O)
        diff_first = diff[:, :, first].rearrange("p t o -> p o t")
        nc.vector.scalar_tensor_tensor(
            out=hid[:, first, :], in0=diff_first, scalar=-1.0, in1=diff_first, op0=ALU.mult, op1=ALU.max
        )
        nc.scalar.activation(out=hid[:, second, :], in_=diff[:, :, second].rearrange("p t o -> p o t"), func=ACT.Abs)
        hid_codes = keep.tile([P, O], U32, name="hid_codes", align_bytes=64)
        hid_plane = keep.tile([P, O], U8, name="hid_plane", align_bytes=64)
        nc.vector.quantize_mx(
            out=hid_codes[:].bitcast(E5M2X4), scales=hid_plane[:], in_=hid[:].rearrange("p o t -> p (o t)")
        )

        for h, (copy, queue) in enumerate(((nc.vector.tensor_copy, nc.sync), (nc.scalar.copy, nc.scalar))):
            rows = slice(h * P, (h + 1) * P)
            bank = psum.tile([P, O], F32, name="y_bank%d" % h)
            nc.tensor.matmul_mx(
                out=bank[:],
                lhsT=vs_gw[:, rows].bitcast(E2M1X4), lhsT_scale=vs_gs[:, rows],
                rhs=hid_codes[:].bitcast(E5M2X4), rhs_scale=hid_plane[:],
                start=True, stop=True,
            )
            y = keep.tile([P, O], F32, name="y%d" % h)
            copy(out=y[:], in_=bank[:])
            queue.dma_start(out=out[rows, :], in_=y[:])
